import numpy as np
import ml_dtypes


def mxq(x, axis, fmt="e4m3"):
    dtype, down = {"e4m3": (ml_dtypes.float8_e4m3fn, 7), "e5m2": (ml_dtypes.float8_e5m2, 14)}[fmt]
    v = np.moveaxis(np.asarray(x, np.float32).astype(ml_dtypes.bfloat16).astype(np.float64), axis, -1)
    blocks = v.reshape(v.shape[:-1] + (-1, 32))
    amax = np.abs(blocks).max(-1, keepdims=True)
    byte = np.maximum(np.where(amax > 0, np.frexp(amax)[1] - 1 + 127, 0) - down, 1)
    scale = np.exp2(byte - 127.0)
    codes = (blocks / scale).astype(np.float32).astype(dtype).astype(np.float64)
    return np.moveaxis((codes * scale).reshape(v.shape), -1, axis)


WIDE = False


def mx_kscale(k):
    if not WIDE:
        return np.ones(k)
    levels = np.array([30, -30])
    if k % 512:
        return np.exp2(np.random.permutation(np.resize(levels, k // 32))).repeat(32)
    a = np.empty((k // 512, 16))
    for p in range(k // 512):
        a[p, :8] = np.random.permutation(np.resize(levels, 8))
        for g in range(8):
            far = levels[np.abs(levels - a[p, g]) >= 10]
            a[p, g + 8] = far[np.random.randint(len(far))]
    return np.exp2(a.ravel()).repeat(32)


def f64(x):
    return np.asarray(x).astype(np.float64)


def striped(idx):
    return np.tile(np.asarray(idx).reshape(-1, 16).T, (8, 1)).astype(np.uint16)


def unstriped(offs):
    return offs[:16].T.reshape(-1).astype(np.int64)


E2M1 = np.array([0.0, 0.5, 1.0, 1.5, 2.0, 3.0, 4.0, 6.0, -0.0, -0.5, -1.0, -1.5, -2.0, -3.0, -4.0, -6.0])


def pack_weight(w, fmt):
    k, n = w.shape
    w = f64(np.asarray(w, np.float32).astype(ml_dtypes.bfloat16)).reshape(k // 32, 32, n)
    amax = np.abs(w).max(1)
    if fmt == "e4m3":
        byte = np.frexp(amax)[1] - 1 + 127 - 7
    else:
        mant, ex = np.frexp(amax / 6.0)
        byte = np.where(mant > 0.5, ex, ex - 1) + 127
    byte = np.clip(np.where(amax > 0, byte, 1), 1, 254)
    scaled = (w * np.exp2(127.0 - byte)[:, None, :]).reshape(k, n).astype(np.float32)
    by_word = np.ascontiguousarray(scaled.reshape(k // 512, 128, 4, n).transpose(0, 1, 3, 2))
    if fmt == "e4m3":
        words = by_word.astype(ml_dtypes.float8_e4m3fn).view(np.uint8)
    else:
        c = by_word.astype(ml_dtypes.float4_e2m1fn).view(np.uint8) & 0xF
        words = (c[..., 0::2] | (c[..., 1::2] << 4)).reshape(k // 512, 128, 2 * n)
    return np.ascontiguousarray(words), np.ascontiguousarray(byte.astype(np.uint8).reshape(k // 512, 16, n))


def unpack_weight(words, scales, fmt):
    g, _, n = scales.shape
    words = np.ascontiguousarray(words).reshape(g, 128, n, -1)
    if fmt == "e4m3":
        vals = words.view(ml_dtypes.float8_e4m3fn).astype(np.float64)
    else:
        nib = np.empty((g, 128, n, 4), np.uint8)
        nib[..., 0::2] = words & 0xF
        nib[..., 1::2] = words >> 4
        vals = E2M1[nib]
    vals = vals * np.repeat(np.exp2(scales.astype(np.float64) - 127.0), 8, axis=1)[..., None]
    return vals.transpose(0, 1, 3, 2).reshape(g * 512, n)


K, T, Z, J, R, C, N, E = 512, 1024, 1024, 256, 512, 512, 256, 1024


def setup_inputs():
    n = np.random.standard_normal
    idx = np.random.permutation(T)[:J]
    idx2 = np.random.permutation(Z)[:J]
    idx3 = np.random.permutation(C)[:J]
    idx4 = np.random.permutation(C)[:J]
    idx5 = np.random.permutation(E)[:J]
    fk = mx_kscale(K)
    fr = mx_kscale(R)
    xtp = pack_weight(n((K, T)) / fk[:, None], "e2m1")
    xop = pack_weight(n((K, Z)) / fk[:, None], "e4m3")
    wp = pack_weight(n((K, R)) * 1 / np.sqrt(K) * fk[:, None] * fr, "e4m3")
    wbp = pack_weight(n((R, N)) * 1 / np.sqrt(R) / fr[:, None], "e2m1")
    return {
        "xt_words": xtp[0],
        "xt_scales": xtp[1],
        "xo_words": xop[0],
        "xo_scales": xop[1],
        "w_words": wp[0],
        "w_scales": wp[1],
        "wb_words": wbp[0],
        "wb_scales": wbp[1],
        "offs": striped(idx),
        "offs2": striped(idx2),
        "offs3": striped(idx3),
        "offs4": striped(idx4),
        "offs5": striped(idx5),
    }


def reference(xt_words, xt_scales, xo_words, xo_scales, w_words, w_scales, wb_words, wb_scales, offs, offs2, offs3, offs4, offs5):
    idx = unstriped(offs)
    idx2 = unstriped(offs2)
    idx3 = unstriped(offs3)
    idx4 = unstriped(offs4)
    idx5 = unstriped(offs5)
    xtu = unpack_weight(xt_words, xt_scales, "e2m1")
    xou = unpack_weight(xo_words, xo_scales, "e4m3")
    wu = unpack_weight(w_words, w_scales, "e4m3")
    wbu = unpack_weight(wb_words, wb_scales, "e2m1")
    xtidxg = xtu[:, idx]
    a = wu.T @ xtidxg
    xoidx2g = xou[:, idx2]
    b = wu.T @ xoidx2g
    pw = np.zeros((R, C))
    pw[:, idx3] = a
    hid = np.abs(pw[:, idx4] - b)
    hidq = mxq(hid, 0, "e5m2")
    p = wbu.T @ hidq
    y = np.zeros((N, E))
    y[:, idx5] = p
    return y

@@ -1,0 +1,150 @@
+from contextlib import ExitStack
+
+import concourse.mybir as mybir
+
+K, T, Z, J, R, C, N, E = 512, 1024, 1024, 256, 512, 512, 256, 1024
+FLOPS = 2 * (2 * K * R * J + R * N * J)
+
+F32 = mybir.dt.float32
+BF16 = mybir.dt.bfloat16
+I32 = mybir.dt.int32
+U32 = mybir.dt.uint32
+U16 = mybir.dt.uint16
+U8 = mybir.dt.uint8
+E4M3 = mybir.dt.float8_e4m3fn_x4
+E5M2 = mybir.dt.float8_e5m2_x4
+E2M1 = mybir.dt.float4_e2m1fn_x4
+COPY = mybir.ActivationFunctionType.Copy
+ABS = mybir.ActivationFunctionType.Abs
+SUB = mybir.AluOpType.subtract
+
+P = 128
+PACK = 4
+HALF = J // 2
+LCOLS = J // 16
+A_ORDER = (1, 0, 3, 2)
+
+
+def load_scales(queues, plane, scales):
+    for q in range(4):
+        queues[q].dma_start(out=plane[32 * q : 32 * q + 4, :].bitcast(I32), in_=scales[0, 4 * q : 4 * q + 4, :].bitcast(I32))
+
+
+def move(nc, on_scalar, out, in_):
+    if on_scalar:
+        nc.scalar.activation(out=out, in_=in_, func=COPY)
+    else:
+        nc.vector.tensor_copy(out=out, in_=in_)
+
+
+def tile_list_oneforboth_board_one_scattered_kernel(tc, xt_words, xt_scales, xo_words, xo_scales, w_words, w_scales, wb_words, wb_scales, offs, offs2, offs3, offs4, offs5, out):
+    nc = tc.nc
+    with ExitStack() as ctx:
+        lists = ctx.enter_context(tc.tile_pool(name="lists", bufs=1))
+        sb = ctx.enter_context(tc.tile_pool(name="sb", bufs=1))
+        ps = ctx.enter_context(tc.psum_pool(name="ps", bufs=1))
+
+        l1 = lists.tile([P, LCOLS], U16, name="l1")
+        l2 = lists.tile([P, LCOLS], U16, name="l2")
+        l3 = lists.tile([P, LCOLS], U16, name="l3")
+        l4 = lists.tile([P, LCOLS], U16, name="l4")
+        l5 = lists.tile([P, LCOLS], U16, name="l5")
+
+        xtw = sb.tile([P, T], U16, name="xtw", align_bytes=64)
+        xts = sb.tile([P, T], U8, name="xts", align_bytes=64)
+        xow = sb.tile([P, Z], U32, name="xow", tag="xow_page", align_bytes=64)
+        xos = sb.tile([P, Z], U8, name="xos", tag="xos_page", align_bytes=64)
+        ww = sb.tile([P, R], U32, name="ww", align_bytes=64)
+        ws = sb.tile([P, R], U8, name="ws", align_bytes=64)
+        wbw = sb.tile([P, 2 * N], U8, name="wbw", align_bytes=64)
+        wbs = sb.tile([P, N], U8, name="wbs", align_bytes=64)
+        boards = [sb.tile([P, C], F32, name=f"board{t}", align_bytes=64) for t in range(PACK)]
+
+        nc.vector.memset(ws[:].bitcast(I32), 0)
+        nc.gpsimd.memset(xts[:].bitcast(I32), 0)
+        nc.vector.memset(xos[:].bitcast(I32), 0)
+        nc.vector.memset(wbs[:].bitcast(I32), 0)
+
+        nc.sync.dma_start(l1[:], offs)
+        nc.sync.dma_start(l3[:], offs3)
+        nc.sync.dma_start(l2[:], offs2)
+        nc.sync.dma_start(out=xtw[:].bitcast(I32), in_=xt_words[0].bitcast(I32))
+        nc.sync.dma_start(out=ww[:].bitcast(I32), in_=w_words[0].rearrange("p n t -> p (n t)").bitcast(I32))
+        load_scales([nc.scalar] * 4, xts, xt_scales)
+        load_scales([nc.sync] * 4, ws, w_scales)
+        nc.sync.dma_start(out=xow[:].bitcast(I32), in_=xo_words[0].rearrange("p n t -> p (n t)").bitcast(I32))
+        load_scales([nc.sync] * 4, xos, xo_scales)
+        nc.sync.dma_start(l4[:], offs4)
+        nc.sync.dma_start(out=wbw[:].bitcast(I32), in_=wb_words[0].bitcast(I32))
+        nc.sync.dma_start(l5[:], offs5)
+        load_scales([nc.sync] * 4, wbs, wb_scales)
+
+        for t in range(PACK):
+            nc.vector.memset(boards[t][:], 0.0)
+
+        gtw = sb.tile([P, J], U16, name="gtw", align_bytes=64)
+        gts = sb.tile([P, J], U8, name="gts", align_bytes=64)
+        gow = sb.tile([P, J], U32, name="gow", align_bytes=64)
+        gos = sb.tile([P, J], U8, name="gos", align_bytes=64)
+        wpw = sb.tile([P, R], U32, name="wpw", align_bytes=64)
+        wps = sb.tile([P, R], U8, name="wps", align_bytes=64)
+
+        nc.vector.tensor_copy(out=gtw[:], in_=xtw[:].indirect(l1[:]))
+        nc.vector.tensor_copy(out=wpw[:].rearrange("p (t m) -> p m t", t=PACK), in_=ww[:].rearrange("p (m t) -> p m t", t=PACK))
+        nc.vector.tensor_copy(out=gts[:], in_=xts[:].indirect(l1[:]))
+        nc.vector.tensor_copy(out=wps[:].rearrange("p (t m) -> p m t", t=PACK), in_=ws[:].rearrange("p (m t) -> p m t", t=PACK))
+
+        a_ps = [ps.tile([P, J], F32, name=f"a_ps{t}", tag=f"bank{t}") for t in range(PACK)]
+        for t in A_ORDER:
+            cols = slice(P * t, P * (t + 1))
+            nc.tensor.matmul_mx(out=a_ps[t][:], lhsT=wpw[:, cols].bitcast(E4M3), lhsT_scale=wps[:, cols],
+                                rhs=gtw[:].bitcast(E2M1), rhs_scale=gts[:], start=True, stop=True)
+
+        nc.vector.tensor_copy(out=gow[:], in_=xow[:].indirect(l2[:]))
+
+        nc.vector.tensor_copy(out=gos[:], in_=xos[:].indirect(l2[:]))
+        a_sb = [sb.tile([P, J], F32, name=f"a_sb{t}", align_bytes=64) for t in range(PACK)]
+        for t in A_ORDER:
+            move(nc, t != 1, a_sb[t][:], a_ps[t][:])
+        for t in range(PACK):
+            move(nc, t % 2 == 0, boards[t][:].indirect(l3[:]), a_sb[t][:])
+
+        pages = [sb.tile([P, E], F32, name=f"page{u}", tag=("xow_page", "xos_page")[u], align_bytes=64) for u in range(2)]
+        for u in range(2):
+            nc.gpsimd.memset(pages[u][:], 0.0)
+
+        b_ps = [ps.tile([P, PACK, HALF], F32, name=f"b_ps{h}", tag=f"bank{PACK + h}") for h in range(2)]
+        for h in range(2):
+            slots = slice(HALF * h, HALF * (h + 1))
+            for t in range(PACK):
+                cols = slice(P * t, P * (t + 1))
+                nc.tensor.matmul_mx(out=b_ps[h][:, t, :], lhsT=wpw[:, cols].bitcast(E4M3), lhsT_scale=wps[:, cols],
+                                    rhs=gow[:, slots].bitcast(E4M3), rhs_scale=gos[:, slots], start=True, stop=True)
+
+        seen = [sb.tile([P, PACK, HALF], F32, name=f"seen{h}", align_bytes=64) for h in range(2)]
+        diff = [sb.tile([P, PACK, HALF], F32, name=f"diff{h}", align_bytes=64) for h in range(2)]
+        hid = [sb.tile([P, HALF, PACK], BF16, name=f"hid{h}", align_bytes=64) for h in range(2)]
+        hw = [sb.tile([P, HALF], U32, name=f"hw{h}", align_bytes=64) for h in range(2)]
+        hs = [sb.tile([P, HALF], U8, name=f"hs{h}", align_bytes=64) for h in range(2)]
+        for h in range(2):
+            entries = slice(LCOLS // 2 * h, LCOLS // 2 * (h + 1))
+            for t in range(PACK):
+                move(nc, t < 2 + h, seen[h][:, t, :], boards[t][:].indirect(l4[:, entries]))
+        for h in range(2):
+            nc.vector.tensor_tensor(out=diff[h][:], in0=seen[h][:], in1=b_ps[h][:], op=SUB)
+        for h in range(2):
+            nc.scalar.activation(out=hid[h][:].rearrange("p (c i) t -> p c t i", i=4),
+                                 in_=diff[h][:].rearrange("p t (c i) -> p c t i", i=4), func=ABS)
+        for h in range(2):
+            nc.vector.quantize_mx(out=hw[h][:].bitcast(E5M2), scales=hs[h][:], in_=hid[h][:].rearrange("p j t -> p (j t)"))
+        for h in range(2):
+            entries = slice(LCOLS // 2 * h, LCOLS // 2 * (h + 1))
+            for u in range(2):
+                p_ps = ps.tile([P, HALF], F32, name=f"p_ps{h}{u}", tag=f"bank{2 * h + u}")
+                nc.tensor.matmul_mx(out=p_ps[:], lhsT=wbw[:, 2 * P * u : 2 * P * (u + 1)].bitcast(E2M1), lhsT_scale=wbs[:, P * u : P * (u + 1)],
+                                    rhs=hw[h][:].bitcast(E5M2), rhs_scale=hs[h][:], start=True, stop=True)
+                p_sb = sb.tile([P, HALF], F32, name=f"p_sb{h}{u}", align_bytes=64)
+                move(nc, u == 1, p_sb[:], p_ps[:])
+                move(nc, u == 0, pages[u][:].indirect(l5[:, entries]), p_sb[:])
+        nc.scalar.dma_start(out=out[0:P, :], in_=pages[0][:])
+        nc.sync.dma_start(out=out[P : 2 * P, :], in_=pages[1][:])

@@ -22,7 +22,7 @@ P = 128
 PACK = 4
 HALF = J // 2
 LCOLS = J // 16
-A_ORDER = (1, 0, 3, 2)
+A_ORDER = (0, 1, 2, 3)
 
 
 def load_scales(queues, plane, scales):
@@ -60,24 +60,24 @@ def tile_list_oneforboth_board_one_scattered_kernel(tc, xt_words, xt_scales, xo_
         wbs = sb.tile([P, N], U8, name="wbs", align_bytes=64)
         boards = [sb.tile([P, C], F32, name=f"board{t}", align_bytes=64) for t in range(PACK)]
 
-        nc.vector.memset(ws[:].bitcast(I32), 0)
-        nc.gpsimd.memset(xts[:].bitcast(I32), 0)
+        nc.vector.memset(xts[:].bitcast(I32), 0)
+        nc.gpsimd.memset(ws[:].bitcast(I32), 0)
         nc.vector.memset(xos[:].bitcast(I32), 0)
         nc.vector.memset(wbs[:].bitcast(I32), 0)
 
         nc.sync.dma_start(l1[:], offs)
-        nc.sync.dma_start(l3[:], offs3)
-        nc.sync.dma_start(l2[:], offs2)
         nc.sync.dma_start(out=xtw[:].bitcast(I32), in_=xt_words[0].bitcast(I32))
+        nc.sync.dma_start(l3[:], offs3)
         nc.sync.dma_start(out=ww[:].bitcast(I32), in_=w_words[0].rearrange("p n t -> p (n t)").bitcast(I32))
-        load_scales([nc.scalar] * 4, xts, xt_scales)
+        nc.sync.dma_start(l2[:], offs2)
+        load_scales([nc.sync] * 4, xts, xt_scales)
         load_scales([nc.sync] * 4, ws, w_scales)
         nc.sync.dma_start(out=xow[:].bitcast(I32), in_=xo_words[0].rearrange("p n t -> p (n t)").bitcast(I32))
         load_scales([nc.sync] * 4, xos, xo_scales)
-        nc.sync.dma_start(l4[:], offs4)
         nc.sync.dma_start(out=wbw[:].bitcast(I32), in_=wb_words[0].bitcast(I32))
         nc.sync.dma_start(l5[:], offs5)
         load_scales([nc.sync] * 4, wbs, wb_scales)
+        nc.sync.dma_start(l4[:], offs4)
 
         for t in range(PACK):
             nc.vector.memset(boards[t][:], 0.0)
@@ -92,11 +92,11 @@ def tile_list_oneforboth_board_one_scattered_kernel(tc, xt_words, xt_scales, xo_
         nc.vector.tensor_copy(out=gtw[:], in_=xtw[:].indirect(l1[:]))
         nc.vector.tensor_copy(out=wpw[:].rearrange("p (t m) -> p m t", t=PACK), in_=ww[:].rearrange("p (m t) -> p m t", t=PACK))
         nc.vector.tensor_copy(out=gts[:], in_=xts[:].indirect(l1[:]))
-        nc.vector.tensor_copy(out=wps[:].rearrange("p (t m) -> p m t", t=PACK), in_=ws[:].rearrange("p (m t) -> p m t", t=PACK))
 
         a_ps = [ps.tile([P, J], F32, name=f"a_ps{t}", tag=f"bank{t}") for t in range(PACK)]
         for t in A_ORDER:
             cols = slice(P * t, P * (t + 1))
+            nc.vector.tensor_copy(out=wps[:, cols], in_=ws[:, t:R:PACK])
             nc.tensor.matmul_mx(out=a_ps[t][:], lhsT=wpw[:, cols].bitcast(E4M3), lhsT_scale=wps[:, cols],
                                 rhs=gtw[:].bitcast(E2M1), rhs_scale=gts[:], start=True, stop=True)
 
@@ -104,9 +104,11 @@ def tile_list_oneforboth_board_one_scattered_kernel(tc, xt_words, xt_scales, xo_
 
         nc.vector.tensor_copy(out=gos[:], in_=xos[:].indirect(l2[:]))
         a_sb = [sb.tile([P, J], F32, name=f"a_sb{t}", align_bytes=64) for t in range(PACK)]
-        for t in A_ORDER:
-            move(nc, t != 1, a_sb[t][:], a_ps[t][:])
+        for t in range(PACK - 1):
+            move(nc, True, a_sb[t][:], a_ps[t][:])
         for t in range(PACK):
+            if t == 2:
+                move(nc, True, a_sb[3][:], a_ps[3][:])
             move(nc, t % 2 == 0, boards[t][:].indirect(l3[:]), a_sb[t][:])
 
         pages = [sb.tile([P, E], F32, name=f"page{u}", tag=("xow_page", "xos_page")[u], align_bytes=64) for u in range(2)]
@@ -129,7 +131,7 @@ def tile_list_oneforboth_board_one_scattered_kernel(tc, xt_words, xt_scales, xo_
         for h in range(2):
             entries = slice(LCOLS // 2 * h, LCOLS // 2 * (h + 1))
             for t in range(PACK):
-                move(nc, t < 2 + h, seen[h][:, t, :], boards[t][:].indirect(l4[:, entries]))
+                move(nc, t % 2 == 0 or (t, h) == (1, 1), seen[h][:, t, :], boards[t][:].indirect(l4[:, entries]))
         for h in range(2):
             nc.vector.tensor_tensor(out=diff[h][:], in0=seen[h][:], in1=b_ps[h][:], op=SUB)
         for h in range(2):
@@ -137,14 +139,16 @@ def tile_list_oneforboth_board_one_scattered_kernel(tc, xt_words, xt_scales, xo_
                                  in_=diff[h][:].rearrange("p t (c i) -> p c t i", i=4), func=ABS)
         for h in range(2):
             nc.vector.quantize_mx(out=hw[h][:].bitcast(E5M2), scales=hs[h][:], in_=hid[h][:].rearrange("p j t -> p (j t)"))
+        p_sb = [sb.tile([P, J], F32, name=f"p_sb{u}", align_bytes=64) for u in range(2)]
         for h in range(2):
             entries = slice(LCOLS // 2 * h, LCOLS // 2 * (h + 1))
+            slots = slice(HALF * h, HALF * (h + 1))
             for u in range(2):
                 p_ps = ps.tile([P, HALF], F32, name=f"p_ps{h}{u}", tag=f"bank{2 * h + u}")
                 nc.tensor.matmul_mx(out=p_ps[:], lhsT=wbw[:, 2 * P * u : 2 * P * (u + 1)].bitcast(E2M1), lhsT_scale=wbs[:, P * u : P * (u + 1)],
                                     rhs=hw[h][:].bitcast(E5M2), rhs_scale=hs[h][:], start=True, stop=True)
-                p_sb = sb.tile([P, HALF], F32, name=f"p_sb{h}{u}", align_bytes=64)
-                move(nc, u == 1, p_sb[:], p_ps[:])
-                move(nc, u == 0, pages[u][:].indirect(l5[:, entries]), p_sb[:])
+                move(nc, h == 0 and u == 0, p_sb[u][:, slots], p_ps[:])
+            move(nc, True, pages[0][:].indirect(l5[:, entries]), p_sb[0][:, slots])
+        move(nc, False, pages[1][:].indirect(l5[:]), p_sb[1][:])
         nc.scalar.dma_start(out=out[0:P, :], in_=pages[0][:])
         nc.sync.dma_start(out=out[P : 2 * P, :], in_=pages[1][:])

@@ -22,7 +22,7 @@ P = 128
 PACK = 4
 HALF = J // 2
 LCOLS = J // 16
-A_ORDER = (0, 1, 2, 3)
+A_ORDER = (1, 0, 2, 3)
 
 
 def load_scales(queues, plane, scales):
@@ -104,7 +104,7 @@ def tile_list_oneforboth_board_one_scattered_kernel(tc, xt_words, xt_scales, xo_
 
         nc.vector.tensor_copy(out=gos[:], in_=xos[:].indirect(l2[:]))
         a_sb = [sb.tile([P, J], F32, name=f"a_sb{t}", align_bytes=64) for t in range(PACK)]
-        for t in range(PACK - 1):
+        for t in A_ORDER[:-1]:
             move(nc, True, a_sb[t][:], a_ps[t][:])
         for t in range(PACK):
             if t == 2:

from contextlib import ExitStack

import concourse.mybir as mybir

K, T, Z, J, R, C, N, E = 512, 1024, 1024, 256, 512, 512, 256, 1024
FLOPS = 2 * (2 * K * R * J + R * N * J)

F32 = mybir.dt.float32
BF16 = mybir.dt.bfloat16
I32 = mybir.dt.int32
U32 = mybir.dt.uint32
U16 = mybir.dt.uint16
U8 = mybir.dt.uint8
E4M3 = mybir.dt.float8_e4m3fn_x4
E5M2 = mybir.dt.float8_e5m2_x4
E2M1 = mybir.dt.float4_e2m1fn_x4
COPY = mybir.ActivationFunctionType.Copy
ABS = mybir.ActivationFunctionType.Abs
SUB = mybir.AluOpType.subtract

P = 128
PACK = 4
HALF = J // 2
LCOLS = J // 16
A_ORDER = (1, 0, 2, 3)


def load_scales(queues, plane, scales):
    for q in range(4):
        queues[q].dma_start(out=plane[32 * q : 32 * q + 4, :].bitcast(I32), in_=scales[0, 4 * q : 4 * q + 4, :].bitcast(I32))


def move(nc, on_scalar, out, in_):
    if on_scalar:
        nc.scalar.activation(out=out, in_=in_, func=COPY)
    else:
        nc.vector.tensor_copy(out=out, in_=in_)


def tile_list_oneforboth_board_one_scattered_kernel(tc, xt_words, xt_scales, xo_words, xo_scales, w_words, w_scales, wb_words, wb_scales, offs, offs2, offs3, offs4, offs5, out):
    nc = tc.nc
    with ExitStack() as ctx:
        lists = ctx.enter_context(tc.tile_pool(name="lists", bufs=1))
        sb = ctx.enter_context(tc.tile_pool(name="sb", bufs=1))
        ps = ctx.enter_context(tc.psum_pool(name="ps", bufs=1))

        l1 = lists.tile([P, LCOLS], U16, name="l1")
        l2 = lists.tile([P, LCOLS], U16, name="l2")
        l3 = lists.tile([P, LCOLS], U16, name="l3")
        l4 = lists.tile([P, LCOLS], U16, name="l4")
        l5 = lists.tile([P, LCOLS], U16, name="l5")

        xtw = sb.tile([P, T], U16, name="xtw", align_bytes=64)
        xts = sb.tile([P, T], U8, name="xts", align_bytes=64)
        xow = sb.tile([P, Z], U32, name="xow", tag="xow_page", align_bytes=64)
        xos = sb.tile([P, Z], U8, name="xos", tag="xos_page", align_bytes=64)
        ww = sb.tile([P, R], U32, name="ww", align_bytes=64)
        ws = sb.tile([P, R], U8, name="ws", align_bytes=64)
        wbw = sb.tile([P, 2 * N], U8, name="wbw", align_bytes=64)
        wbs = sb.tile([P, N], U8, name="wbs", align_bytes=64)
        boards = [sb.tile([P, C], F32, name=f"board{t}", align_bytes=64) for t in range(PACK)]

        nc.vector.memset(xts[:].bitcast(I32), 0)
        nc.gpsimd.memset(ws[:].bitcast(I32), 0)
        nc.vector.memset(xos[:].bitcast(I32), 0)
        nc.vector.memset(wbs[:].bitcast(I32), 0)

        nc.sync.dma_start(l1[:], offs)
        nc.sync.dma_start(out=xtw[:].bitcast(I32), in_=xt_words[0].bitcast(I32))
        nc.sync.dma_start(l3[:], offs3)
        nc.sync.dma_start(out=ww[:].bitcast(I32), in_=w_words[0].rearrange("p n t -> p (n t)").bitcast(I32))
        nc.sync.dma_start(l2[:], offs2)
        load_scales([nc.sync] * 4, xts, xt_scales)
        load_scales([nc.sync] * 4, ws, w_scales)
        nc.sync.dma_start(out=xow[:].bitcast(I32), in_=xo_words[0].rearrange("p n t -> p (n t)").bitcast(I32))
        load_scales([nc.sync] * 4, xos, xo_scales)
        nc.sync.dma_start(out=wbw[:].bitcast(I32), in_=wb_words[0].bitcast(I32))
        nc.sync.dma_start(l5[:], offs5)
        load_scales([nc.sync] * 4, wbs, wb_scales)
        nc.sync.dma_start(l4[:], offs4)

        for t in range(PACK):
            nc.vector.memset(boards[t][:], 0.0)

        gtw = sb.tile([P, J], U16, name="gtw", align_bytes=64)
        gts = sb.tile([P, J], U8, name="gts", align_bytes=64)
        gow = sb.tile([P, J], U32, name="gow", align_bytes=64)
        gos = sb.tile([P, J], U8, name="gos", align_bytes=64)
        wpw = sb.tile([P, R], U32, name="wpw", align_bytes=64)
        wps = sb.tile([P, R], U8, name="wps", align_bytes=64)

        nc.vector.tensor_copy(out=gtw[:], in_=xtw[:].indirect(l1[:]))
        nc.vector.tensor_copy(out=wpw[:].rearrange("p (t m) -> p m t", t=PACK), in_=ww[:].rearrange("p (m t) -> p m t", t=PACK))
        nc.vector.tensor_copy(out=gts[:], in_=xts[:].indirect(l1[:]))

        a_ps = [ps.tile([P, J], F32, name=f"a_ps{t}", tag=f"bank{t}") for t in range(PACK)]
        for t in A_ORDER:
            cols = slice(P * t, P * (t + 1))
            nc.vector.tensor_copy(out=wps[:, cols], in_=ws[:, t:R:PACK])
            nc.tensor.matmul_mx(out=a_ps[t][:], lhsT=wpw[:, cols].bitcast(E4M3), lhsT_scale=wps[:, cols],
                                rhs=gtw[:].bitcast(E2M1), rhs_scale=gts[:], start=True, stop=True)

        nc.vector.tensor_copy(out=gow[:], in_=xow[:].indirect(l2[:]))

        nc.vector.tensor_copy(out=gos[:], in_=xos[:].indirect(l2[:]))
        a_sb = [sb.tile([P, J], F32, name=f"a_sb{t}", align_bytes=64) for t in range(PACK)]
        for t in A_ORDER[:-1]:
            move(nc, True, a_sb[t][:], a_ps[t][:])
        for t in range(PACK):
            if t == 2:
                move(nc, True, a_sb[3][:], a_ps[3][:])
            move(nc, t % 2 == 0, boards[t][:].indirect(l3[:]), a_sb[t][:])

        pages = [sb.tile([P, E], F32, name=f"page{u}", tag=("xow_page", "xos_page")[u], align_bytes=64) for u in range(2)]
        for u in range(2):
            nc.gpsimd.memset(pages[u][:], 0.0)

        b_ps = [ps.tile([P, PACK, HALF], F32, name=f"b_ps{h}", tag=f"bank{PACK + h}") for h in range(2)]
        for h in range(2):
            slots = slice(HALF * h, HALF * (h + 1))
            for t in range(PACK):
                cols = slice(P * t, P * (t + 1))
                nc.tensor.matmul_mx(out=b_ps[h][:, t, :], lhsT=wpw[:, cols].bitcast(E4M3), lhsT_scale=wps[:, cols],
                                    rhs=gow[:, slots].bitcast(E4M3), rhs_scale=gos[:, slots], start=True, stop=True)

        seen = [sb.tile([P, PACK, HALF], F32, name=f"seen{h}", align_bytes=64) for h in range(2)]
        diff = [sb.tile([P, PACK, HALF], F32, name=f"diff{h}", align_bytes=64) for h in range(2)]
        hid = [sb.tile([P, HALF, PACK], BF16, name=f"hid{h}", align_bytes=64) for h in range(2)]
        hw = [sb.tile([P, HALF], U32, name=f"hw{h}", align_bytes=64) for h in range(2)]
        hs = [sb.tile([P, HALF], U8, name=f"hs{h}", align_bytes=64) for h in range(2)]
        for h in range(2):
            entries = slice(LCOLS // 2 * h, LCOLS // 2 * (h + 1))
            for t in range(PACK):
                move(nc, t % 2 == 0 or (t, h) == (1, 1), seen[h][:, t, :], boards[t][:].indirect(l4[:, entries]))
        for h in range(2):
            nc.vector.tensor_tensor(out=diff[h][:], in0=seen[h][:], in1=b_ps[h][:], op=SUB)
        for h in range(2):
            nc.scalar.activation(out=hid[h][:].rearrange("p (c i) t -> p c t i", i=4),
                                 in_=diff[h][:].rearrange("p t (c i) -> p c t i", i=4), func=ABS)
        for h in range(2):
            nc.vector.quantize_mx(out=hw[h][:].bitcast(E5M2), scales=hs[h][:], in_=hid[h][:].rearrange("p j t -> p (j t)"))
        p_sb = [sb.tile([P, J], F32, name=f"p_sb{u}", align_bytes=64) for u in range(2)]
        for h in range(2):
            entries = slice(LCOLS // 2 * h, LCOLS // 2 * (h + 1))
            slots = slice(HALF * h, HALF * (h + 1))
            for u in range(2):
                p_ps = ps.tile([P, HALF], F32, name=f"p_ps{h}{u}", tag=f"bank{2 * h + u}")
                nc.tensor.matmul_mx(out=p_ps[:], lhsT=wbw[:, 2 * P * u : 2 * P * (u + 1)].bitcast(E2M1), lhsT_scale=wbs[:, P * u : P * (u + 1)],
                                    rhs=hw[h][:].bitcast(E5M2), rhs_scale=hs[h][:], start=True, stop=True)
                move(nc, h == 0 and u == 0, p_sb[u][:, slots], p_ps[:])
            move(nc, True, pages[0][:].indirect(l5[:, entries]), p_sb[0][:, slots])
        move(nc, False, pages[1][:].indirect(l5[:]), p_sb[1][:])
        nc.scalar.dma_start(out=out[0:P, :], in_=pages[0][:])
        nc.sync.dma_start(out=out[P : 2 * P, :], in_=pages[1][:])
